import numpy as np
CORES = [2,5,10,13,18,21,26,29,34,37,42,45]
N = 12
PERM = [[0,3],[1,2],[2,4],[3,7],[4,5],[5,0],[6,10],[7,6],[8,9],[9,11],[10,1],[11,8]]
def setup_inputs(rng):
    return {"x": rng.standard_normal((N, 128, 256), dtype=np.float32)}
def reference(x):
    y = np.empty_like(x)
    for s, d in PERM:
        y[d] = x[s]
    return {"y": y}

@@ -1,0 +1,58 @@
+SCRATCH = {
+    "src": ("sbuf", [128, 256], "float32"),
+    "land": ("sbuf", [128, 256], "float32"),
+}
+SEMAPHORES = ["loaded", "read", "arrived", "stored"]
+
+
+def _engines(mask):
+    return bin(mask).count("1")
+
+
+def _helper(src, dst, group, topo):
+    base = topo.chip(src) * topo.CORES_PER_CHIP
+    for c in range(base, base + topo.CORES_PER_CHIP):
+        if c not in group and topo.die(c) == topo.die(src) and topo.may_write(c, dst):
+            return c
+    return None
+
+
+def _routes(T, topo):
+    group = list(T.cores)
+    paths = []
+    for s, d in T.tables["PERM"]:
+        a, b = group[s], group[d]
+        if topo.may_write(a, b):
+            paths.append([a, b])
+        else:
+            paths.append([a, _helper(a, b, group, topo), b])
+    return paths
+
+
+def _send(g, T, topo, core, nxt, buf):
+    rid, pid, _se = topo.addr(nxt)
+    m = topo.mask(core, nxt)
+    g.remote_dma(T.land[:], buf[:], T.sem.arrived, T.sem.read, pid, rid, m)
+    return _engines(m)
+
+
+def rank_program(g, core, T, topo):
+    for path in _routes(T, topo):
+        if core not in path:
+            continue
+        k = path.index(core)
+        if k == 0:
+            g.sync.dma_start(T.src[:], T.x[:]).then_inc(T.sem.loaded, 16)
+            g.wait_ge(T.sem.loaded, 16)
+            n = _send(g, T, topo, core, path[1], T.src)
+            g.wait_ge(T.sem.read, n)
+        elif k == len(path) - 1:
+            n = _engines(topo.mask(path[k - 1], core))
+            g.scalar.wait_ge(T.sem.arrived, n)
+            g.scalar.dma_start(T.y[:], T.land[:]).then_inc(T.sem.stored, 16)
+            g.scalar.wait_ge(T.sem.stored, 16)
+        else:
+            n = _engines(topo.mask(path[k - 1], core))
+            g.wait_ge(T.sem.arrived, n)
+            n = _send(g, T, topo, core, path[k + 1], T.land)
+            g.wait_ge(T.sem.read, n)

@@ -1,6 +1,6 @@
 SCRATCH = {
-    "src": ("sbuf", [128, 256], "float32"),
-    "land": ("sbuf", [128, 256], "float32"),
+    "src": ("dram", [128, 256], "float32"),
+    "land": ("dram", [128, 256], "float32"),
 }
 SEMAPHORES = ["loaded", "read", "arrived", "stored"]
 

SCRATCH = {
    "src": ("dram", [128, 256], "float32"),
    "land": ("dram", [128, 256], "float32"),
}
SEMAPHORES = ["loaded", "read", "arrived", "stored"]


def _engines(mask):
    return bin(mask).count("1")


def _helper(src, dst, group, topo):
    base = topo.chip(src) * topo.CORES_PER_CHIP
    for c in range(base, base + topo.CORES_PER_CHIP):
        if c not in group and topo.die(c) == topo.die(src) and topo.may_write(c, dst):
            return c
    return None


def _routes(T, topo):
    group = list(T.cores)
    paths = []
    for s, d in T.tables["PERM"]:
        a, b = group[s], group[d]
        if topo.may_write(a, b):
            paths.append([a, b])
        else:
            paths.append([a, _helper(a, b, group, topo), b])
    return paths


def _send(g, T, topo, core, nxt, buf):
    rid, pid, _se = topo.addr(nxt)
    m = topo.mask(core, nxt)
    g.remote_dma(T.land[:], buf[:], T.sem.arrived, T.sem.read, pid, rid, m)
    return _engines(m)


def rank_program(g, core, T, topo):
    for path in _routes(T, topo):
        if core not in path:
            continue
        k = path.index(core)
        if k == 0:
            g.sync.dma_start(T.src[:], T.x[:]).then_inc(T.sem.loaded, 16)
            g.wait_ge(T.sem.loaded, 16)
            n = _send(g, T, topo, core, path[1], T.src)
            g.wait_ge(T.sem.read, n)
        elif k == len(path) - 1:
            n = _engines(topo.mask(path[k - 1], core))
            g.scalar.wait_ge(T.sem.arrived, n)
            g.scalar.dma_start(T.y[:], T.land[:]).then_inc(T.sem.stored, 16)
            g.scalar.wait_ge(T.sem.stored, 16)
        else:
            n = _engines(topo.mask(path[k - 1], core))
            g.wait_ge(T.sem.arrived, n)
            n = _send(g, T, topo, core, path[k + 1], T.land)
            g.wait_ge(T.sem.read, n)
